import numpy as np, ml_dtypes
CORES = [51,54,179,182]
N = 4
TOK, K, FT = 128, 2, 2
ROUTE = [[[1,3],[1,3],[1,2],[0,2],[0,3],[2,3],[1,3],[1,3],[1,2],[1,2],[1,3],[1,3],[1,3],[0,1],[0,2],[0,2],[0,1],[0,3],[0,1],[1,2],[0,3],[0,1],[0,2],[0,2],[0,3],[0,1],[1,2],[0,1],[0,2],[0,3],[0,3],[0,3],[2,3],[1,3],[1,2],[0,1],[1,3],[1,3],[0,2],[2,3],[0,2],[1,3],[1,2],[2,3],[0,1],[2,3],[0,1],[1,3],[1,2],[1,3],[1,3],[1,2],[2,3],[1,2],[0,1],[0,1],[1,3],[2,3],[1,3],[0,3],[0,3],[1,2],[0,3],[1,2],[1,2],[0,3],[1,2],[1,3],[1,3],[2,3],[0,3],[1,3],[0,1],[0,3],[0,1],[0,1],[0,3],[0,3],[0,1],[1,2],[1,3],[2,3],[0,2],[0,2],[2,3],[0,3],[1,2],[0,2],[1,2],[0,3],[2,3],[1,3],[1,2],[2,3],[0,2],[0,2],[2,3],[0,1],[1,3],[0,1],[0,1],[1,2],[1,2],[1,3],[0,2],[2,3],[0,2],[0,3],[0,3],[1,2],[0,1],[1,3],[0,3],[0,1],[0,2],[1,2],[0,2],[1,2],[2,3],[0,3],[0,1],[0,3],[1,2],[0,3],[0,1],[0,1],[1,3],[0,1]],[[1,3],[2,3],[0,2],[2,3],[0,3],[0,1],[0,1],[1,3],[0,2],[2,3],[1,3],[0,1],[1,2],[1,3],[0,1],[0,3],[1,3],[0,3],[0,1],[0,3],[1,3],[2,3],[0,1],[1,2],[1,3],[2,3],[1,3],[1,2],[0,1],[0,1],[2,3],[0,1],[0,1],[1,2],[1,2],[1,2],[0,2],[0,1],[1,3],[1,2],[0,3],[1,2],[0,1],[0,1],[1,2],[1,3],[0,2],[0,1],[0,3],[1,3],[1,3],[0,3],[0,3],[0,1],[2,3],[0,2],[0,3],[0,3],[0,1],[1,3],[0,3],[2,3],[0,1],[0,3],[2,3],[0,1],[0,1],[1,3],[1,2],[0,1],[0,1],[0,3],[1,3],[0,1],[0,3],[0,2],[1,2],[0,1],[2,3],[1,3],[0,2],[0,2],[1,2],[2,3],[0,3],[0,2],[0,1],[0,2],[1,2],[0,1],[2,3],[1,3],[2,3],[0,3],[1,3],[1,3],[0,1],[0,3],[0,1],[0,1],[1,3],[0,2],[1,3],[0,1],[0,2],[2,3],[1,3],[0,1],[0,3],[0,1],[1,2],[2,3],[2,3],[0,1],[1,3],[0,3],[1,2],[1,2],[0,2],[1,3],[0,2],[0,2],[0,2],[0,2],[0,1],[0,1],[0,3],[2,3]],[[2,3],[0,2],[1,3],[0,1],[2,3],[0,2],[1,2],[0,1],[0,3],[1,2],[0,2],[0,1],[2,3],[1,2],[1,3],[2,3],[0,3],[2,3],[2,3],[0,1],[1,3],[1,3],[0,1],[0,2],[1,3],[2,3],[1,3],[1,2],[2,3],[0,2],[1,3],[0,1],[0,2],[2,3],[0,2],[0,1],[0,3],[1,2],[2,3],[0,3],[1,2],[1,3],[0,3],[0,2],[0,1],[0,3],[0,2],[0,1],[2,3],[1,3],[0,1],[0,3],[2,3],[1,3],[0,1],[1,3],[1,2],[2,3],[1,3],[2,3],[0,2],[0,3],[1,3],[1,3],[0,1],[0,1],[1,3],[0,3],[0,2],[0,1],[1,3],[0,2],[2,3],[2,3],[0,2],[1,2],[0,3],[0,3],[0,3],[2,3],[1,3],[0,2],[0,3],[0,2],[1,2],[2,3],[1,3],[2,3],[2,3],[1,3],[2,3],[0,1],[1,3],[0,1],[0,3],[0,3],[0,3],[1,3],[0,1],[0,3],[1,3],[0,3],[0,2],[1,2],[1,3],[0,3],[0,2],[0,2],[2,3],[0,2],[0,3],[0,2],[1,3],[1,2],[1,3],[1,3],[0,1],[2,3],[1,2],[2,3],[2,3],[0,3],[2,3],[1,3],[0,2],[2,3],[1,3],[0,2]],[[1,2],[1,3],[2,3],[2,3],[0,2],[1,3],[1,2],[0,3],[1,2],[1,2],[0,2],[0,2],[0,1],[0,3],[1,3],[0,3],[0,1],[0,3],[1,2],[1,2],[1,2],[1,2],[0,1],[2,3],[1,3],[1,3],[1,3],[1,3],[2,3],[1,3],[0,3],[0,3],[1,3],[0,3],[2,3],[2,3],[1,2],[1,3],[0,1],[2,3],[0,1],[1,2],[1,2],[0,2],[1,3],[0,2],[0,1],[0,3],[0,3],[0,2],[0,1],[2,3],[0,3],[1,3],[0,2],[0,1],[0,2],[0,2],[2,3],[0,3],[0,3],[0,1],[1,2],[0,2],[2,3],[0,2],[2,3],[1,2],[1,3],[0,2],[0,2],[1,2],[1,2],[2,3],[0,2],[0,1],[0,3],[2,3],[1,3],[2,3],[1,3],[2,3],[2,3],[1,3],[0,1],[0,1],[1,2],[0,2],[0,1],[1,2],[0,3],[0,1],[0,3],[1,2],[0,2],[2,3],[1,2],[0,3],[2,3],[1,2],[0,1],[0,1],[0,1],[0,1],[1,2],[0,1],[0,2],[0,1],[0,1],[2,3],[1,2],[0,2],[0,2],[1,2],[0,2],[0,2],[0,3],[1,3],[0,1],[0,3],[1,3],[2,3],[2,3],[0,3],[2,3],[2,3],[2,3],[1,2]]]
def setup_inputs(rng):
    return {"x": rng.standard_normal((N, 128, TOK), dtype=np.float32).astype(ml_dtypes.bfloat16), "gate": (0.5 * rng.integers(1, 4, size=(N, K, TOK)) * (2 * rng.integers(0, 2, size=(N, K, TOK)) - 1)).astype(np.float32).astype(ml_dtypes.bfloat16), "w1": (rng.standard_normal((N, 128, FT * 128), dtype=np.float32) / 8).astype(ml_dtypes.bfloat16), "w2": (rng.standard_normal((N, 128, FT * 128), dtype=np.float32) / 8).astype(ml_dtypes.bfloat16)}
def setup_inputs_big(rng):
    d = setup_inputs(rng)
    for k in ("x", "gate", "w1", "w2"): d[k] = (d[k].astype(np.float32) * 1024.0).astype(d[k].dtype)
    return d
def setup_inputs_small(rng):
    d = setup_inputs(rng)
    for k in ("x", "gate", "w1", "w2"): d[k] = (d[k].astype(np.float32) * (1 / 1024.0)).astype(d[k].dtype)
    return d
def reference(x, gate, w1, w2):
    X, GATE, W1, W2 = x.astype(np.float64), gate.astype(np.float64), w1.astype(np.float64), w2.astype(np.float64)
    y = np.zeros((N, 128, TOK))
    for r in range(N):
        for t in range(TOK):
            for i, e in enumerate(ROUTE[r][t]):
                hid = np.maximum(W1[e].T @ X[r][:, t], 0.0)
                y[r][:, t] += GATE[r][i, t] * sum(W2[e][:, 128 * f:128 * f + 128].T @ hid[128 * f:128 * f + 128] for f in range(FT))
    return {"y": y.astype(ml_dtypes.bfloat16)}

@@ -1,0 +1,209 @@
+from concourse.bass import DstId, RemoteDMATransfer
+from concourse.mybir import AluOpType
+
+_N = 4
+_W = 512
+
+SCRATCH = {
+    "wsb": ("sbuf", [128, _N * _W], "bfloat16"),
+    "xsb": ("sbuf", [128, 128], "bfloat16"),
+    "gsb": ("sbuf", [128, 256], "bfloat16"),
+    "zsb": ("sbuf", [128, 256], "bfloat16"),
+    "one": ("sbuf", [128, 128], "bfloat16"),
+    "neg": ("sbuf", [128, 128], "bfloat16"),
+    "tsb": ("sbuf", [128, 256], "bfloat16"),
+    "rsb": ("sbuf", [128, _N * 256], "bfloat16"),
+    "hsb": ("sbuf", [128, _N * 256], "bfloat16"),
+    "ysb": ("sbuf", [128, 128], "bfloat16"),
+    "u0": ("psum", [128, 512], "float32"),
+    "u1": ("psum", [128, 512], "float32"),
+    "u2": ("psum", [128, 512], "float32"),
+    "u3": ("psum", [128, 512], "float32"),
+    "rp": ("psum", [128, 512], "float32"),
+    "cp": ("psum", [128, 512], "float32"),
+    "yp": ("psum", [128, 512], "float32"),
+}
+SEMAPHORES = (["ld_w1", "ld_w2", "ld_x", "ld_g", "st_y", "sent", "m_zero", "m_one", "m_rp", "s_pt", "s_t", "s_c", "s_y", "s_o"]
+              + ["a1_%d" % s for s in range(_N)] + ["a2_%d" % s for s in range(_N)]
+              + ["s_u%d" % e for e in range(_N)] + ["s_r%d" % e for e in range(_N)] + ["s_h%d" % e for e in range(_N)])
+
+
+def _runs(seq):
+    out, t0 = [], 0
+    for t in range(1, len(seq) + 1):
+        if t == len(seq) or seq[t] != seq[t0]:
+            out.append((seq[t0], t0, t))
+            t0 = t
+    return out
+
+
+def _engines(mask):
+    return bin(mask).count("1")
+
+
+def rank_program(g, core, T, topo):
+    rank = T.rank_of(core)
+    if rank is None:
+        return
+    TOK, K, FT = T.tables["TOK"], T.tables["K"], T.tables["FT"]
+    route = T.tables["ROUTE"][rank]
+    sem = T.sem
+    pe, ve = g.tensor, g.vector
+    H = FT * 128
+
+    def w1(e, f=None):
+        if f is None:
+            return T.wsb[:, e * _W:e * _W + H]
+        return T.wsb[:, e * _W + 128 * f:e * _W + 128 * f + 128]
+
+    def w2(e, f=None):
+        if f is None:
+            return T.wsb[:, e * _W + H:e * _W + 2 * H]
+        return T.wsb[:, e * _W + H + 128 * f:e * _W + H + 128 * f + 128]
+
+    def same_chip(a, b):
+        return topo.host(a) == topo.host(b) and topo.chip(a) == topo.chip(b)
+
+    peers = [s for s in range(_N) if s != rank]
+    near = [s for s in peers if same_chip(T.cores[s], core)]
+    far = [s for s in peers if not same_chip(T.cores[s], core)]
+    far.sort(key=lambda s: (topo.die(T.cores[s]) != topo.die(core), s))
+    far_mask = 0
+    for s in far:
+        far_mask = topo.mask(core, T.cores[s]) if far_mask == 0 else far_mask & topo.mask(core, T.cores[s])
+    near_mask = 0
+    for s in near:
+        near_mask = topo.mask(core, T.cores[s]) if near_mask == 0 else near_mask & topo.mask(core, T.cores[s])
+    if near_mask & ~far_mask:
+        near_mask &= ~far_mask
+
+    def ids(ranks):
+        out = []
+        for s in ranks:
+            rid, pid = topo.addr(T.cores[s], core)
+            out.append(DstId(rid=rid, pnc=pid))
+        return out
+
+    g.sync.dma_start(w1(rank), T.w1[:, :]).then_inc(sem.ld_w1, 16)
+    g.scalar.dma_start(w2(rank), T.w2[:, :]).then_inc(sem.ld_w2, 16)
+    g.sync.dma_start(T.xsb[:, :], T.x[:, :]).then_inc(sem.ld_x, 16)
+    g.scalar.dma_start(T.gsb[0:1, 0:K * TOK], T.gate[:, :]).then_inc(sem.ld_g, 16)
+
+    sent = 0
+    if far:
+        g.wait_ge(sem.ld_w1, 16)
+        g.remote_dma_fused([RemoteDMATransfer(dst_ids=ids(far), dma_engine_mask=far_mask, remote_sem=sem["a1_%d" % rank],
+                                              srcs=[w1(rank)], dsts=[w1(rank) for _ in far])], local_sem=sem.sent)
+        g.wait_ge(sem.ld_w2, 16)
+        g.remote_dma_fused([RemoteDMATransfer(dst_ids=ids(far), dma_engine_mask=far_mask, remote_sem=sem["a2_%d" % rank],
+                                              srcs=[w2(rank)], dsts=[w2(rank) for _ in far])], local_sem=sem.sent)
+        sent += 2 * _engines(far_mask)
+    if near:
+        g.wait_ge(sem.ld_w1, 16)
+        g.wait_ge(sem.ld_w2, 16)
+        both = T.wsb[:, rank * _W:rank * _W + 2 * H]
+        g.remote_dma_fused([RemoteDMATransfer(dst_ids=ids(near), dma_engine_mask=near_mask, remote_sem=sem["a1_%d" % rank],
+                                              srcs=[both], dsts=[both for _ in near])], local_sem=sem.sent)
+        sent += _engines(near_mask)
+
+    far_n, near_n = _engines(far_mask), _engines(near_mask)
+
+    rows, paints, base = [], [], {}
+    for i in range(K):
+        rs = _runs([route[t][i] for t in range(TOK)])
+        cnt = {}
+        for e, _a, _b in rs:
+            cnt[e] = cnt.get(e, 0) + 1
+        base[i] = max(sorted(cnt), key=lambda e: cnt[e])
+        for e in sorted(cnt):
+            if e != base[i]:
+                rows.append((i, e))
+        for e, a, b in rs:
+            if e != base[i]:
+                paints.append((rows.index((i, e)), i, a, b))
+    nblk = (len(rows) + 3) // 4
+
+    def row_at(j):
+        return 32 * (j % 4), TOK * (j // 4)
+
+    terms = {e: [] for e in range(_N)}
+    for i in range(K):
+        terms[base[i]].append((T.one[0:1, :], T.gsb[0:1, i * TOK:(i + 1) * TOK]))
+    for j, (i, e) in enumerate(rows):
+        p, c = row_at(j)
+        terms[e].append((T.one[p:p + 1, :], T.tsb[p:p + 1, c:c + TOK]))
+        terms[base[i]].append((T.neg[p:p + 1, :], T.tsb[p:p + 1, c:c + TOK]))
+    n_bc = sum(len(v) for v in terms.values())
+
+    order1 = [rank] + far + near
+    order2 = [rank] + near + far
+    U = {e: T["u%d" % e] for e in range(_N)}
+
+    ve.memset(T.rp[:, 0:max(nblk, 1) * TOK], 0.0).then_inc(sem.m_rp, 1)
+    ve.memset(T.one[:, :], 1.0).then_inc(sem.m_one, 1)
+    ve.memset(T.neg[:, :], -1.0).then_inc(sem.m_one, 1)
+    ve.memset(T.zsb[:, 0:H], 0.0).then_inc(sem.m_zero, 1)
+    ve.wait_ge(sem.m_zero, 1)
+
+    def relu(e):
+        ve.wait_ge(sem["s_u%d" % e], FT)
+        ve.tensor_tensor(T.rsb[:, e * H:(e + 1) * H], U[e][:, 0:H], T.zsb[:, 0:H], AluOpType.max).then_inc(sem["s_r%d" % e], 1)
+
+    def scale(e):
+        ve.wait_ge(sem["s_r%d" % e], 1)
+        for f in range(FT):
+            c = e * H + 128 * f
+            ve.tensor_tensor(T.hsb[:, c:c + 128], T.rsb[:, c:c + 128], T.cp[:, e * TOK:(e + 1) * TOK],
+                             AluOpType.mult).then_inc(sem["s_h%d" % e], 1)
+
+    relu(rank)
+    ve.wait_ge(sem.s_pt, len(paints))
+    ve.tensor_copy(T.tsb[:, 0:max(nblk, 1) * TOK], T.rp[:, 0:max(nblk, 1) * TOK]).then_inc(sem.s_t, 1)
+    ve.wait_ge(sem.s_c, n_bc)
+    scale(rank)
+    for e in order1[1:]:
+        relu(e)
+        scale(e)
+    ve.wait_ge(sem.s_y, _N * FT)
+    ve.tensor_copy(T.ysb[:, :], T.yp[:, 0:TOK]).then_inc(sem.s_o, 1)
+
+    def mm1(e):
+        for f in range(FT):
+            pe.matmul(U[e][:, 128 * f:128 * f + TOK], w1(e, f), T.xsb[:, :], True, True).then_inc(sem["s_u%d" % e], 1)
+
+    pe.wait_ge(sem.ld_w1, 16)
+    pe.wait_ge(sem.ld_x, 16)
+    mm1(rank)
+    pe.wait_ge(sem.m_rp, 1)
+    pe.wait_ge(sem.m_one, 2)
+    pe.wait_ge(sem.ld_g, 16)
+    for j, i, a, b in paints:
+        p, c = row_at(j)
+        pe.matmul(T.rp[p:p + 1, c + a:c + b], T.one[0:1, 0:1], T.gsb[0:1, i * TOK + a:i * TOK + b], True, True).then_inc(sem.s_pt, 1)
+    pe.wait_ge(sem.s_t, 1)
+    nb = 0
+    for e in range(_N):
+        for k, (lhsT, rhs) in enumerate(terms[e]):
+            if nb:
+                pe.wait_ge(sem.s_c, nb)
+            pe.matmul(T.cp[:, e * TOK:(e + 1) * TOK], lhsT, rhs, k == 0, k == len(terms[e]) - 1).then_inc(sem.s_c, 1)
+            nb += 1
+    for e in order1[1:]:
+        pe.wait_ge(sem["a1_%d" % e], far_n if e in far else near_n)
+        mm1(e)
+    done = 0
+    for e in order2:
+        if e == rank:
+            pe.wait_ge(sem.ld_w2, 16)
+        elif e in far:
+            pe.wait_ge(sem["a2_%d" % e], far_n)
+        pe.wait_ge(sem["s_h%d" % e], FT)
+        for f in range(FT):
+            c = e * H + 128 * f
+            pe.matmul(T.yp[:, 0:TOK], w2(e, f), T.hsb[:, c:c + 128], done == 0, done == _N * FT - 1).then_inc(sem.s_y, 1)
+            done += 1
+
+    g.sync.wait_ge(sem.s_o, 1)
+    g.sync.dma_start(T.y[:, :], T.ysb[:, :]).then_inc(sem.st_y, 16)
+    g.sync.wait_ge(sem.st_y, 16)
+    g.wait_ge(sem.sent, sent)

@@ -10,8 +10,7 @@ SCRATCH = {
     "gsb": ("sbuf", [128, 256], "bfloat16"),
     "zsb": ("sbuf", [128, 256], "bfloat16"),
     "one": ("sbuf", [128, 128], "bfloat16"),
-    "neg": ("sbuf", [128, 128], "bfloat16"),
-    "tsb": ("sbuf", [128, 256], "bfloat16"),
+    "tsb": ("sbuf", [128, 128], "bfloat16"),
     "rsb": ("sbuf", [128, _N * 256], "bfloat16"),
     "hsb": ("sbuf", [128, _N * 256], "bfloat16"),
     "ysb": ("sbuf", [128, 128], "bfloat16"),
@@ -19,12 +18,13 @@ SCRATCH = {
     "u1": ("psum", [128, 512], "float32"),
     "u2": ("psum", [128, 512], "float32"),
     "u3": ("psum", [128, 512], "float32"),
-    "rp": ("psum", [128, 512], "float32"),
-    "cp": ("psum", [128, 512], "float32"),
-    "yp": ("psum", [128, 512], "float32"),
+    "ry": ("psum", [128, 512], "float32"),
+    "c1": ("psum", [128, 512], "float32"),
+    "c2": ("psum", [128, 512], "float32"),
+    "c3": ("psum", [128, 512], "float32"),
 }
-SEMAPHORES = (["ld_w1", "ld_w2", "ld_x", "ld_g", "st_y", "sent", "m_zero", "m_one", "m_rp", "s_pt", "s_t", "s_c", "s_y", "s_o"]
-              + ["a1_%d" % s for s in range(_N)] + ["a2_%d" % s for s in range(_N)]
+SEMAPHORES = (["ld_w1", "ld_w2", "ld_x", "ld_g", "st_y", "sent", "m_zero", "m_one", "m_rp", "s_pt", "s_t", "s_y", "s_o"]
+              + ["a1_%d" % s for s in range(_N)] + ["a2_%d" % s for s in range(_N)] + ["s_c%d" % e for e in range(_N)]
               + ["s_u%d" % e for e in range(_N)] + ["s_r%d" % e for e in range(_N)] + ["s_h%d" % e for e in range(_N)])
 
 
@@ -68,80 +68,53 @@ def rank_program(g, core, T, topo):
     near = [s for s in peers if same_chip(T.cores[s], core)]
     far = [s for s in peers if not same_chip(T.cores[s], core)]
     far.sort(key=lambda s: (topo.die(T.cores[s]) != topo.die(core), s))
-    far_mask = 0
-    for s in far:
-        far_mask = topo.mask(core, T.cores[s]) if far_mask == 0 else far_mask & topo.mask(core, T.cores[s])
-    near_mask = 0
-    for s in near:
-        near_mask = topo.mask(core, T.cores[s]) if near_mask == 0 else near_mask & topo.mask(core, T.cores[s])
-    if near_mask & ~far_mask:
-        near_mask &= ~far_mask
+    partner, other = far[0], far[1]
+    far_mask = topo.mask(core, T.cores[partner])
+    chip_mask = topo.mask(core, T.cores[near[0]])
+    near_mask = chip_mask & ~far_mask
+    far_n, near_n, chip_n = _engines(far_mask), _engines(near_mask), _engines(chip_mask)
 
-    def ids(ranks):
-        out = []
-        for s in ranks:
+    def send(ap, to, mask, name):
+        dst = []
+        for s in to:
             rid, pid = topo.addr(T.cores[s], core)
-            out.append(DstId(rid=rid, pnc=pid))
-        return out
+            dst.append(DstId(rid=rid, pnc=pid))
+        g.remote_dma_fused([RemoteDMATransfer(dst_ids=dst, dma_engine_mask=mask, remote_sem=sem[name],
+                                              srcs=[ap], dsts=[ap for _ in to])], local_sem=sem.sent)
+        return _engines(mask)
 
     g.sync.dma_start(w1(rank), T.w1[:, :]).then_inc(sem.ld_w1, 16)
+    g.scalar.dma_start(T.gsb[0:1, 0:K * TOK], T.gate[:, :]).then_inc(sem.ld_g, 16)
     g.scalar.dma_start(w2(rank), T.w2[:, :]).then_inc(sem.ld_w2, 16)
     g.sync.dma_start(T.xsb[:, :], T.x[:, :]).then_inc(sem.ld_x, 16)
-    g.scalar.dma_start(T.gsb[0:1, 0:K * TOK], T.gate[:, :]).then_inc(sem.ld_g, 16)
 
     sent = 0
-    if far:
-        g.wait_ge(sem.ld_w1, 16)
-        g.remote_dma_fused([RemoteDMATransfer(dst_ids=ids(far), dma_engine_mask=far_mask, remote_sem=sem["a1_%d" % rank],
-                                              srcs=[w1(rank)], dsts=[w1(rank) for _ in far])], local_sem=sem.sent)
-        g.wait_ge(sem.ld_w2, 16)
-        g.remote_dma_fused([RemoteDMATransfer(dst_ids=ids(far), dma_engine_mask=far_mask, remote_sem=sem["a2_%d" % rank],
-                                              srcs=[w2(rank)], dsts=[w2(rank) for _ in far])], local_sem=sem.sent)
-        sent += 2 * _engines(far_mask)
-    if near:
-        g.wait_ge(sem.ld_w1, 16)
-        g.wait_ge(sem.ld_w2, 16)
-        both = T.wsb[:, rank * _W:rank * _W + 2 * H]
-        g.remote_dma_fused([RemoteDMATransfer(dst_ids=ids(near), dma_engine_mask=near_mask, remote_sem=sem["a1_%d" % rank],
-                                              srcs=[both], dsts=[both for _ in near])], local_sem=sem.sent)
-        sent += _engines(near_mask)
+    g.wait_ge(sem.ld_w1, 16)
+    sent += send(w1(rank), [partner], far_mask, "a1_%d" % rank)
+    g.wait_ge(sem.ld_w2, 16)
+    sent += send(w2(rank), [partner], far_mask, "a2_%d" % rank)
+    sent += send(T.wsb[:, rank * _W:rank * _W + 2 * H], near, near_mask, "a1_%d" % rank)
+    g.wait_ge(sem["a1_%d" % partner], far_n)
+    sent += send(w1(partner), near, near_mask, "a1_%d" % partner)
+    g.wait_ge(sem["a2_%d" % partner], far_n)
+    sent += send(w2(partner), near, chip_mask, "a2_%d" % partner)
+    n1 = {partner: far_n, other: near_n, near[0]: near_n}
+    n2 = {partner: far_n, other: chip_n}
 
-    far_n, near_n = _engines(far_mask), _engines(near_mask)
-
-    rows, paints, base = [], [], {}
+    paints = []
     for i in range(K):
-        rs = _runs([route[t][i] for t in range(TOK)])
-        cnt = {}
-        for e, _a, _b in rs:
-            cnt[e] = cnt.get(e, 0) + 1
-        base[i] = max(sorted(cnt), key=lambda e: cnt[e])
-        for e in sorted(cnt):
-            if e != base[i]:
-                rows.append((i, e))
-        for e, a, b in rs:
-            if e != base[i]:
-                paints.append((rows.index((i, e)), i, a, b))
-    nblk = (len(rows) + 3) // 4
-
-    def row_at(j):
-        return 32 * (j % 4), TOK * (j // 4)
-
-    terms = {e: [] for e in range(_N)}
-    for i in range(K):
-        terms[base[i]].append((T.one[0:1, :], T.gsb[0:1, i * TOK:(i + 1) * TOK]))
-    for j, (i, e) in enumerate(rows):
-        p, c = row_at(j)
-        terms[e].append((T.one[p:p + 1, :], T.tsb[p:p + 1, c:c + TOK]))
-        terms[base[i]].append((T.neg[p:p + 1, :], T.tsb[p:p + 1, c:c + TOK]))
-    n_bc = sum(len(v) for v in terms.values())
-
-    order1 = [rank] + far + near
-    order2 = [rank] + near + far
+        for e, a, b in _runs([route[t][i] for t in range(TOK)]):
+            paints.append((e, i, a, b))
+    order1 = [rank, partner] + near + [other]
+    order2 = [rank] + near + [partner, other]
     U = {e: T["u%d" % e] for e in range(_N)}
+    RP, YP = T.ry[:, 0:TOK], T.ry[:, TOK:2 * TOK]
+    C = {rank: T.ry[:, 2 * TOK:3 * TOK]}
+    for k, e in enumerate(order1[1:]):
+        C[e] = T["c%d" % (k + 1)][:, 0:TOK]
 
-    ve.memset(T.rp[:, 0:max(nblk, 1) * TOK], 0.0).then_inc(sem.m_rp, 1)
+    ve.memset(RP, 0.0).then_inc(sem.m_rp, 1)
     ve.memset(T.one[:, :], 1.0).then_inc(sem.m_one, 1)
-    ve.memset(T.neg[:, :], -1.0).then_inc(sem.m_one, 1)
     ve.memset(T.zsb[:, 0:H], 0.0).then_inc(sem.m_zero, 1)
     ve.wait_ge(sem.m_zero, 1)
 
@@ -151,56 +124,47 @@ def rank_program(g, core, T, topo):
 
     def scale(e):
         ve.wait_ge(sem["s_r%d" % e], 1)
+        ve.wait_ge(sem["s_c%d" % e], 1)
         for f in range(FT):
             c = e * H + 128 * f
-            ve.tensor_tensor(T.hsb[:, c:c + 128], T.rsb[:, c:c + 128], T.cp[:, e * TOK:(e + 1) * TOK],
-                             AluOpType.mult).then_inc(sem["s_h%d" % e], 1)
+            ve.tensor_tensor(T.hsb[:, c:c + 128], T.rsb[:, c:c + 128], C[e], AluOpType.mult).then_inc(sem["s_h%d" % e], 1)
 
-    relu(rank)
     ve.wait_ge(sem.s_pt, len(paints))
-    ve.tensor_copy(T.tsb[:, 0:max(nblk, 1) * TOK], T.rp[:, 0:max(nblk, 1) * TOK]).then_inc(sem.s_t, 1)
-    ve.wait_ge(sem.s_c, n_bc)
-    scale(rank)
-    for e in order1[1:]:
+    ve.tensor_copy(T.tsb[:, :], RP).then_inc(sem.s_t, 1)
+    for e in order1:
         relu(e)
         scale(e)
     ve.wait_ge(sem.s_y, _N * FT)
-    ve.tensor_copy(T.ysb[:, :], T.yp[:, 0:TOK]).then_inc(sem.s_o, 1)
+    ve.tensor_copy(T.ysb[:, :], YP).then_inc(sem.s_o, 1)
 
     def mm1(e):
         for f in range(FT):
             pe.matmul(U[e][:, 128 * f:128 * f + TOK], w1(e, f), T.xsb[:, :], True, True).then_inc(sem["s_u%d" % e], 1)
 
+    pe.wait_ge(sem.m_rp, 1)
+    pe.wait_ge(sem.m_one, 1)
+    pe.wait_ge(sem.ld_g, 16)
+    for e, i, a, b in paints:
+        pe.matmul(T.ry[32 * e:32 * e + 1, a:b], T.one[0:1, 0:1], T.gsb[0:1, i * TOK + a:i * TOK + b], True, True).then_inc(sem.s_pt, 1)
     pe.wait_ge(sem.ld_w1, 16)
     pe.wait_ge(sem.ld_x, 16)
     mm1(rank)
-    pe.wait_ge(sem.m_rp, 1)
-    pe.wait_ge(sem.m_one, 2)
-    pe.wait_ge(sem.ld_g, 16)
-    for j, i, a, b in paints:
-        p, c = row_at(j)
-        pe.matmul(T.rp[p:p + 1, c + a:c + b], T.one[0:1, 0:1], T.gsb[0:1, i * TOK + a:i * TOK + b], True, True).then_inc(sem.s_pt, 1)
     pe.wait_ge(sem.s_t, 1)
-    nb = 0
-    for e in range(_N):
-        for k, (lhsT, rhs) in enumerate(terms[e]):
-            if nb:
-                pe.wait_ge(sem.s_c, nb)
-            pe.matmul(T.cp[:, e * TOK:(e + 1) * TOK], lhsT, rhs, k == 0, k == len(terms[e]) - 1).then_inc(sem.s_c, 1)
-            nb += 1
+    for e in order1:
+        pe.matmul(C[e], T.one[32 * e:32 * e + 1, :], T.tsb[32 * e:32 * e + 1, :], True, True).then_inc(sem["s_c%d" % e], 1)
     for e in order1[1:]:
-        pe.wait_ge(sem["a1_%d" % e], far_n if e in far else near_n)
+        pe.wait_ge(sem["a1_%d" % e], n1[e])
         mm1(e)
     done = 0
     for e in order2:
         if e == rank:
             pe.wait_ge(sem.ld_w2, 16)
-        elif e in far:
-            pe.wait_ge(sem["a2_%d" % e], far_n)
+        elif e in n2:
+            pe.wait_ge(sem["a2_%d" % e], n2[e])
         pe.wait_ge(sem["s_h%d" % e], FT)
         for f in range(FT):
             c = e * H + 128 * f
-            pe.matmul(T.yp[:, 0:TOK], w2(e, f), T.hsb[:, c:c + 128], done == 0, done == _N * FT - 1).then_inc(sem.s_y, 1)
+            pe.matmul(YP, w2(e, f), T.hsb[:, c:c + 128], done == 0, done == _N * FT - 1).then_inc(sem.s_y, 1)
             done += 1
 
     g.sync.wait_ge(sem.s_o, 1)

from concourse.bass import DstId, RemoteDMATransfer
from concourse.mybir import AluOpType

_N = 4
_W = 512

SCRATCH = {
    "wsb": ("sbuf", [128, _N * _W], "bfloat16"),
    "xsb": ("sbuf", [128, 128], "bfloat16"),
    "gsb": ("sbuf", [128, 256], "bfloat16"),
    "zsb": ("sbuf", [128, 256], "bfloat16"),
    "one": ("sbuf", [128, 128], "bfloat16"),
    "tsb": ("sbuf", [128, 128], "bfloat16"),
    "rsb": ("sbuf", [128, _N * 256], "bfloat16"),
    "hsb": ("sbuf", [128, _N * 256], "bfloat16"),
    "ysb": ("sbuf", [128, 128], "bfloat16"),
    "u0": ("psum", [128, 512], "float32"),
    "u1": ("psum", [128, 512], "float32"),
    "u2": ("psum", [128, 512], "float32"),
    "u3": ("psum", [128, 512], "float32"),
    "ry": ("psum", [128, 512], "float32"),
    "c1": ("psum", [128, 512], "float32"),
    "c2": ("psum", [128, 512], "float32"),
    "c3": ("psum", [128, 512], "float32"),
}
SEMAPHORES = (["ld_w1", "ld_w2", "ld_x", "ld_g", "st_y", "sent", "m_zero", "m_one", "m_rp", "s_pt", "s_t", "s_y", "s_o"]
              + ["a1_%d" % s for s in range(_N)] + ["a2_%d" % s for s in range(_N)] + ["s_c%d" % e for e in range(_N)]
              + ["s_u%d" % e for e in range(_N)] + ["s_r%d" % e for e in range(_N)] + ["s_h%d" % e for e in range(_N)])


def _runs(seq):
    out, t0 = [], 0
    for t in range(1, len(seq) + 1):
        if t == len(seq) or seq[t] != seq[t0]:
            out.append((seq[t0], t0, t))
            t0 = t
    return out


def _engines(mask):
    return bin(mask).count("1")


def rank_program(g, core, T, topo):
    rank = T.rank_of(core)
    if rank is None:
        return
    TOK, K, FT = T.tables["TOK"], T.tables["K"], T.tables["FT"]
    route = T.tables["ROUTE"][rank]
    sem = T.sem
    pe, ve = g.tensor, g.vector
    H = FT * 128

    def w1(e, f=None):
        if f is None:
            return T.wsb[:, e * _W:e * _W + H]
        return T.wsb[:, e * _W + 128 * f:e * _W + 128 * f + 128]

    def w2(e, f=None):
        if f is None:
            return T.wsb[:, e * _W + H:e * _W + 2 * H]
        return T.wsb[:, e * _W + H + 128 * f:e * _W + H + 128 * f + 128]

    def same_chip(a, b):
        return topo.host(a) == topo.host(b) and topo.chip(a) == topo.chip(b)

    peers = [s for s in range(_N) if s != rank]
    near = [s for s in peers if same_chip(T.cores[s], core)]
    far = [s for s in peers if not same_chip(T.cores[s], core)]
    far.sort(key=lambda s: (topo.die(T.cores[s]) != topo.die(core), s))
    partner, other = far[0], far[1]
    far_mask = topo.mask(core, T.cores[partner])
    chip_mask = topo.mask(core, T.cores[near[0]])
    near_mask = chip_mask & ~far_mask
    far_n, near_n, chip_n = _engines(far_mask), _engines(near_mask), _engines(chip_mask)

    def send(ap, to, mask, name):
        dst = []
        for s in to:
            rid, pid = topo.addr(T.cores[s], core)
            dst.append(DstId(rid=rid, pnc=pid))
        g.remote_dma_fused([RemoteDMATransfer(dst_ids=dst, dma_engine_mask=mask, remote_sem=sem[name],
                                              srcs=[ap], dsts=[ap for _ in to])], local_sem=sem.sent)
        return _engines(mask)

    g.sync.dma_start(w1(rank), T.w1[:, :]).then_inc(sem.ld_w1, 16)
    g.scalar.dma_start(T.gsb[0:1, 0:K * TOK], T.gate[:, :]).then_inc(sem.ld_g, 16)
    g.scalar.dma_start(w2(rank), T.w2[:, :]).then_inc(sem.ld_w2, 16)
    g.sync.dma_start(T.xsb[:, :], T.x[:, :]).then_inc(sem.ld_x, 16)

    sent = 0
    g.wait_ge(sem.ld_w1, 16)
    sent += send(w1(rank), [partner], far_mask, "a1_%d" % rank)
    g.wait_ge(sem.ld_w2, 16)
    sent += send(w2(rank), [partner], far_mask, "a2_%d" % rank)
    sent += send(T.wsb[:, rank * _W:rank * _W + 2 * H], near, near_mask, "a1_%d" % rank)
    g.wait_ge(sem["a1_%d" % partner], far_n)
    sent += send(w1(partner), near, near_mask, "a1_%d" % partner)
    g.wait_ge(sem["a2_%d" % partner], far_n)
    sent += send(w2(partner), near, chip_mask, "a2_%d" % partner)
    n1 = {partner: far_n, other: near_n, near[0]: near_n}
    n2 = {partner: far_n, other: chip_n}

    paints = []
    for i in range(K):
        for e, a, b in _runs([route[t][i] for t in range(TOK)]):
            paints.append((e, i, a, b))
    order1 = [rank, partner] + near + [other]
    order2 = [rank] + near + [partner, other]
    U = {e: T["u%d" % e] for e in range(_N)}
    RP, YP = T.ry[:, 0:TOK], T.ry[:, TOK:2 * TOK]
    C = {rank: T.ry[:, 2 * TOK:3 * TOK]}
    for k, e in enumerate(order1[1:]):
        C[e] = T["c%d" % (k + 1)][:, 0:TOK]

    ve.memset(RP, 0.0).then_inc(sem.m_rp, 1)
    ve.memset(T.one[:, :], 1.0).then_inc(sem.m_one, 1)
    ve.memset(T.zsb[:, 0:H], 0.0).then_inc(sem.m_zero, 1)
    ve.wait_ge(sem.m_zero, 1)

    def relu(e):
        ve.wait_ge(sem["s_u%d" % e], FT)
        ve.tensor_tensor(T.rsb[:, e * H:(e + 1) * H], U[e][:, 0:H], T.zsb[:, 0:H], AluOpType.max).then_inc(sem["s_r%d" % e], 1)

    def scale(e):
        ve.wait_ge(sem["s_r%d" % e], 1)
        ve.wait_ge(sem["s_c%d" % e], 1)
        for f in range(FT):
            c = e * H + 128 * f
            ve.tensor_tensor(T.hsb[:, c:c + 128], T.rsb[:, c:c + 128], C[e], AluOpType.mult).then_inc(sem["s_h%d" % e], 1)

    ve.wait_ge(sem.s_pt, len(paints))
    ve.tensor_copy(T.tsb[:, :], RP).then_inc(sem.s_t, 1)
    for e in order1:
        relu(e)
        scale(e)
    ve.wait_ge(sem.s_y, _N * FT)
    ve.tensor_copy(T.ysb[:, :], YP).then_inc(sem.s_o, 1)

    def mm1(e):
        for f in range(FT):
            pe.matmul(U[e][:, 128 * f:128 * f + TOK], w1(e, f), T.xsb[:, :], True, True).then_inc(sem["s_u%d" % e], 1)

    pe.wait_ge(sem.m_rp, 1)
    pe.wait_ge(sem.m_one, 1)
    pe.wait_ge(sem.ld_g, 16)
    for e, i, a, b in paints:
        pe.matmul(T.ry[32 * e:32 * e + 1, a:b], T.one[0:1, 0:1], T.gsb[0:1, i * TOK + a:i * TOK + b], True, True).then_inc(sem.s_pt, 1)
    pe.wait_ge(sem.ld_w1, 16)
    pe.wait_ge(sem.ld_x, 16)
    mm1(rank)
    pe.wait_ge(sem.s_t, 1)
    for e in order1:
        pe.matmul(C[e], T.one[32 * e:32 * e + 1, :], T.tsb[32 * e:32 * e + 1, :], True, True).then_inc(sem["s_c%d" % e], 1)
    for e in order1[1:]:
        pe.wait_ge(sem["a1_%d" % e], n1[e])
        mm1(e)
    done = 0
    for e in order2:
        if e == rank:
            pe.wait_ge(sem.ld_w2, 16)
        elif e in n2:
            pe.wait_ge(sem["a2_%d" % e], n2[e])
        pe.wait_ge(sem["s_h%d" % e], FT)
        for f in range(FT):
            c = e * H + 128 * f
            pe.matmul(YP, w2(e, f), T.hsb[:, c:c + 128], done == 0, done == _N * FT - 1).then_inc(sem.s_y, 1)
            done += 1

    g.sync.wait_ge(sem.s_o, 1)
    g.sync.dma_start(T.y[:, :], T.ysb[:, :]).then_inc(sem.st_y, 16)
    g.sync.wait_ge(sem.st_y, 16)
    g.wait_ge(sem.sent, sent)
